import numpy as np
import ml_dtypes


def mxq(x, axis, fmt="e4m3"):
    dtype, down = {"e4m3": (ml_dtypes.float8_e4m3fn, 7), "e5m2": (ml_dtypes.float8_e5m2, 14)}[fmt]
    v = np.moveaxis(np.asarray(x, np.float32).astype(ml_dtypes.bfloat16).astype(np.float64), axis, -1)
    blocks = v.reshape(v.shape[:-1] + (-1, 32))
    amax = np.abs(blocks).max(-1, keepdims=True)
    byte = np.maximum(np.where(amax > 0, np.frexp(amax)[1] - 1 + 127, 0) - down, 1)
    scale = np.exp2(byte - 127.0)
    codes = (blocks / scale).astype(np.float32).astype(dtype).astype(np.float64)
    return np.moveaxis((codes * scale).reshape(v.shape), -1, axis)


WIDE = False


def mx_kscale(k):
    if not WIDE:
        return np.ones(k)
    levels = np.array([10, -10, 5, -5, 0])
    if k % 512:
        return np.exp2(np.random.permutation(np.resize(levels, k // 32))).repeat(32)
    a = np.empty((k // 512, 16))
    for p in range(k // 512):
        a[p, :8] = np.random.permutation(np.resize(levels, 8))
        for g in range(8):
            far = levels[np.abs(levels - a[p, g]) >= 10]
            a[p, g + 8] = far[np.random.randint(len(far))]
    return np.exp2(a.ravel()).repeat(32)


def f64(x):
    return np.asarray(x).astype(np.float64)


def striped(idx):
    return np.tile(idx.reshape(-1, 16).T, (8, 1)).astype(np.uint16)


def unstriped(offs):
    return offs[:16].T.reshape(-1).astype(np.int64)


E2M1 = np.array([0.0, 0.5, 1.0, 1.5, 2.0, 3.0, 4.0, 6.0, -0.0, -0.5, -1.0, -1.5, -2.0, -3.0, -4.0, -6.0])


def pack_weight(w, fmt):
    k, n = w.shape
    w = f64(np.asarray(w, np.float32).astype(ml_dtypes.bfloat16)).reshape(k // 32, 32, n)
    amax = np.abs(w).max(1)
    if fmt == "e4m3":
        byte = np.frexp(amax)[1] - 1 + 127 - 7
    else:
        mant, ex = np.frexp(amax / 6.0)
        byte = np.where(mant > 0.5, ex, ex - 1) + 127
    byte = np.clip(np.where(amax > 0, byte, 1), 1, 254)
    scaled = (w * np.exp2(127.0 - byte)[:, None, :]).reshape(k, n).astype(np.float32)
    by_word = np.ascontiguousarray(scaled.reshape(k // 512, 128, 4, n).transpose(0, 1, 3, 2))
    if fmt == "e4m3":
        words = by_word.astype(ml_dtypes.float8_e4m3fn).view(np.uint8)
    else:
        c = by_word.astype(ml_dtypes.float4_e2m1fn).view(np.uint8) & 0xF
        words = (c[..., 0::2] | (c[..., 1::2] << 4)).reshape(k // 512, 128, 2 * n)
    return np.ascontiguousarray(words), np.ascontiguousarray(byte.astype(np.uint8).reshape(k // 512, 16, n))


def unpack_weight(words, scales, fmt):
    g, _, n = scales.shape
    words = np.ascontiguousarray(words).reshape(g, 128, n, -1)
    if fmt == "e4m3":
        vals = words.view(ml_dtypes.float8_e4m3fn).astype(np.float64)
    else:
        nib = np.empty((g, 128, n, 4), np.uint8)
        nib[..., 0::2] = words & 0xF
        nib[..., 1::2] = words >> 4
        vals = E2M1[nib]
    vals = vals * np.repeat(np.exp2(scales.astype(np.float64) - 127.0), 8, axis=1)[..., None]
    return vals.transpose(0, 1, 3, 2).reshape(g * 512, n)


def gelu(v):
    return 0.5 * v * (1.0 + np.tanh(np.sqrt(2.0 / np.pi) * (v + 0.044715 * v**3)))


K, T, S, H, T2, P, N = 512, 4096, 1024, 1024, 2048, 1024, 768


def setup_inputs():
    n = np.random.standard_normal
    s = mx_kscale(K)[:, None]
    u = mx_kscale(H)[:, None]
    d = {}
    d["tab_words"], d["tab_scales"] = pack_weight(n((K, T)) * s, "e4m3")
    d["offs"] = striped(np.random.permutation(T)[:S])
    d["offs2"] = striped(np.random.permutation(T2)[:S])
    d["offs3"] = striped(np.random.permutation(T2)[:P])
    d["offs4"] = striped(np.random.permutation(T2)[:P])
    d["w1"] = (n((K, H)) / K**0.5 / s).astype(np.float32)
    d["w2_words"], d["w2_scales"] = pack_weight(n((K, H)) / K**0.5 / s, "e2m1")
    d["w3"] = (n((K, H)) / K**0.5 / s).astype(np.float32)
    d["gain"] = (0.8 * np.exp(0.3 * n(H)) * u[:, 0]).astype(np.float32)
    d["wgs"] = np.exp(0.3 * n((128, S))).astype(np.float32)
    d["page0"] = (n((H, T2)) * u).astype(np.float32)
    d["b"] = (0.8 * n(H) * u[:, 0]).astype(np.float32)
    d["w4_words"], d["w4_scales"] = pack_weight(1.6 * n((H, N)) / H**0.5 / u, "e4m3")
    d["wgo"] = np.exp(0.3 * n((128, P))).astype(np.float32)
    d["page1"] = n((N, T2)).astype(np.float32)
    return d


def reference(tab_words, tab_scales, offs, offs2, offs3, offs4, w1, w2_words, w2_scales, w3, gain, wgs, page0, b, w4_words, w4_scales, wgo, page1):
    v = unpack_weight(tab_words, tab_scales, "e4m3")[:, unstriped(offs)]
    h1 = mxq(f64(w1), 0, "e4m3").T @ v
    h2 = unpack_weight(w2_words, w2_scales, "e2m1").T @ v
    h3 = mxq(f64(w3), 0, "e4m3").T @ v
    h = f64(gain)[:, None] * (h1 + h2 * h3)
    page = f64(page0).copy()
    page[:, unstriped(offs2)] = np.tile(f64(wgs), (H // 128, 1)) * h
    x = page[:, unstriped(offs3)] + f64(b)[:, None]
    e = unpack_weight(w4_words, w4_scales, "e4m3").T @ mxq(x, 0, "e4m3")
    y = np.log(np.abs(e) + 1.0)
    out = f64(page1).copy()
    out[:, unstriped(offs4)] = np.tile(f64(wgo), (N // 128, 1)) * y
    return out

@@ -1,0 +1,271 @@
+from contextlib import ExitStack
+
+import concourse.mybir as mybir
+
+K, T, S, H, T2, M, N = 512, 4096, 1024, 1024, 2048, 1024, 768
+FLOPS = 2 * 3 * K * H * S + 2 * H * N * M
+
+F32 = mybir.dt.float32
+BF16 = mybir.dt.bfloat16
+I32 = mybir.dt.int32
+U32 = mybir.dt.uint32
+U16 = mybir.dt.uint16
+U8 = mybir.dt.uint8
+FP8X4 = mybir.dt.float8_e4m3fn_x4
+FP4X4 = mybir.dt.float4_e2m1fn_x4
+ALU = mybir.AluOpType
+ACT = mybir.ActivationFunctionType
+
+P = 128
+PACK = 4
+BANK = 512
+LIST_COLS = BANK // 16
+ROW_TILES = H // P
+OUT_TILES = N // P
+
+
+def tile_list_cellar_transfer_page_kernel(
+    tc, tab_words, tab_scales, offs, offs2, offs3, offs4, w1, w2_words, w2_scales, w3, gain, wgs, page0, b,
+    w4_words, w4_scales, wgo, page1, out,
+):
+    nc = tc.nc
+    with ExitStack() as ctx:
+        keep = ctx.enter_context(tc.tile_pool(name="keep", bufs=1))
+        ring = ctx.enter_context(tc.tile_pool(name="ring", bufs=2))
+        psum = ctx.enter_context(tc.psum_pool(name="psum", bufs=2))
+
+        def half(h):
+            return slice(h * BANK, (h + 1) * BANK)
+
+        def list_half(tile, h):
+            return tile[:, h * LIST_COLS : (h + 1) * LIST_COLS]
+
+        def load_list(src, name):
+            tile = keep.tile([P, S // 16], U16, name=name)
+            nc.sync.dma_start(tile[:], src)
+            return tile
+
+        def load_scale_rows(queue, tile, src):
+            for q in range(4):
+                queue.dma_start(
+                    out=tile[32 * q : 32 * q + 4].bitcast(I32),
+                    in_=src[:, 4 * q : 4 * q + 4, :].rearrange("a q c -> q a c").bitcast(I32),
+                )
+
+        def load_weight_half(src, a, name):
+            raw = ring.tile([P, PACK, BANK], F32, name=name, tag="big", bufs=6)
+            nc.sync.dma_start(out=raw[:], in_=src[:, half(a)].rearrange("(p i) c -> p i c", i=PACK))
+            return raw
+
+        def load_page(src, name, tag):
+            tile = ring.tile([P, T2], F32, name=name, tag=tag, bufs=6)
+            nc.sync.dma_start(out=tile[:], in_=src)
+            return tile
+
+        page0_rows = page0.rearrange("(a p t) c -> a t p c", a=2, t=PACK)
+        wgs_rows = wgs.rearrange("(p t) j -> p t j", t=PACK)
+
+        tab_s = keep.tile([P, 1, T], U8, align_bytes=64)
+        nc.vector.memset(tab_s[:].bitcast(I32), 0)
+        w2_s_raw = keep.tile([P, 1, H], U8, align_bytes=64)
+        nc.gpsimd.memset(w2_s_raw[:].bitcast(I32), 0)
+        gain_t = keep.tile([P, 2, PACK], F32)
+        nc.gpsimd.dma_start(out=gain_t[:], in_=gain.rearrange("(a p t) -> p a t", a=2, t=PACK))
+        b_t = keep.tile([P, 2, PACK], F32)
+        nc.gpsimd.dma_start(out=b_t[:], in_=b.rearrange("(a p t) -> p a t", a=2, t=PACK))
+        w4_s = keep.tile([P, 2, N], U8, align_bytes=64)
+        nc.gpsimd.memset(w4_s[:].bitcast(I32), 0)
+
+        idx1 = load_list(offs, "idx1")
+        w2_raw = keep.tile([P, 2 * H], U8, align_bytes=64)
+        nc.sync.dma_start(out=w2_raw[:].bitcast(I32), in_=w2_words[0].bitcast(I32))
+        tab_w = keep.tile([P, T], U32, align_bytes=64)
+        nc.sync.dma_start(out=tab_w[:].bitcast(I32), in_=tab_words[0].rearrange("p t i -> p (t i)").bitcast(I32))
+        load_scale_rows(nc.sync, tab_s, tab_scales)
+        raw = {}
+        raw[0, 0] = load_weight_half(w1, 0, "w1_raw0")
+        load_scale_rows(nc.sync, w2_s_raw, w2_scales)
+        raw[1, 0] = load_weight_half(w3, 0, "w3_raw0")
+        wgs_first = keep.tile([P, S], F32)
+        for q in range(4):
+            nc.sync.dma_start(out=wgs_first[32 * q : 32 * q + 32, :], in_=wgs_rows[:, 0, :])
+        idx2 = load_list(offs2, "idx2")
+        pages = [load_page(page0_rows[0, 0], "page0_0", "page0")]
+        wgs_rest = keep.tile([P, PACK - 1, S], F32, tag="wgs_rest")
+        for q in range(4):
+            nc.sync.dma_start(out=wgs_rest[32 * q : 32 * q + 32], in_=wgs_rows[:, 1:PACK, :])
+        pages.append(load_page(page0_rows[0, 1], "page0_1", "page0"))
+        idx3 = load_list(offs3, "idx3")
+        pages.append(load_page(page0_rows[0, 2], "page0_2", "page0"))
+        raw[0, 1] = load_weight_half(w1, 1, "w1_raw1")
+        raw[1, 1] = load_weight_half(w3, 1, "w3_raw1")
+        for i in range(3, 6):
+            pages.append(load_page(page0_rows[i // PACK, i % PACK], "page0_%d" % i, "page0"))
+        w4_w = keep.tile([P, 2, N], U32, align_bytes=64)
+        nc.sync.dma_start(out=w4_w[:].bitcast(I32), in_=w4_words.rearrange("a p c i -> p a (c i)").bitcast(I32))
+        load_scale_rows(nc.sync, w4_s, w4_scales)
+        wgo_t = keep.tile([P, M], F32)
+        nc.sync.dma_start(out=wgo_t[:], in_=wgo)
+        idx4 = load_list(offs4, "idx4")
+
+        w2_w = keep.tile([P, 2 * H], U8, align_bytes=64)
+        nc.vector.tensor_copy(
+            out=w2_w[:].rearrange("p (a t m e) -> p a t m e", a=2, t=PACK, e=2),
+            in_=w2_raw[:].rearrange("p (a m t e) -> p a t m e", a=2, t=PACK, e=2),
+        )
+        w2_s = keep.tile([P, H], U8, align_bytes=64)
+
+        def deal_w2_scales(a):
+            nc.vector.tensor_copy(
+                out=w2_s[:, half(a)].rearrange("p (t m) -> p t m", t=PACK),
+                in_=w2_s_raw[:, 0, half(a)].rearrange("p (m t) -> p t m", t=PACK),
+            )
+
+        v_w = [keep.tile([P, BANK], U32, name="v_w%d" % h, align_bytes=64) for h in range(2)]
+        v_s = [keep.tile([P, BANK], U8, name="v_s%d" % h, align_bytes=64) for h in range(2)]
+        for h in range(2):
+            nc.vector.tensor_copy(v_w[h][:], tab_w[:].indirect(list_half(idx1, h)))
+            nc.vector.tensor_copy(v_s[h][:], tab_s[:, 0, :].indirect(list_half(idx1, h)))
+            if h == 0:
+                deal_w2_scales(0)
+
+        wq = {}
+
+        for which in range(2):
+            for a in range(2):
+                wq[which, a] = (
+                    keep.tile([P, BANK], U32, name="wq_w%d%d" % (which, a), align_bytes=64),
+                    keep.tile([P, BANK], U8, name="wq_s%d%d" % (which, a), align_bytes=64),
+                )
+
+        def quantise_weight(which, a, t0, t1, copy):
+            grouped = ring.tile([P, t1 - t0, P, PACK], BF16, name="w_grouped%d" % min(t1 - t0, 2), align_bytes=64)
+            codes, scales = wq[which, a]
+            src = raw[which, a][:].rearrange("p i (m t) -> p t m i", t=PACK)
+            for t in range(t0, t1):
+                copy(out=grouped[:, t - t0], in_=src[:, t])
+            nc.vector.quantize_mx(
+                out=codes[:, t0 * P : t1 * P].bitcast(FP8X4),
+                scales=scales[:, t0 * P : t1 * P],
+                in_=grouped[:].rearrange("p t m i -> p (t m i)"),
+            )
+
+        def first_stage(i):
+            a, t = divmod(i, PACK)
+            weights = wgs_first[:] if t == 0 else wgs_rest[:, t - 1, :]
+            h_tile = keep.tile([P, S], F32, name="h_tile", tag="h_tile%d" % (i % 2))
+            cols = slice(t * P, (t + 1) * P)
+            gain_col = gain_t[:, a, t : t + 1]
+            for h in range(2):
+                h1 = psum.tile([P, BANK], F32, name="h1")
+                h2 = psum.tile([P, BANK], F32, name="h2")
+                h3 = psum.tile([P, BANK], F32, name="h3")
+                moving = dict(rhs=v_w[h][:].bitcast(FP8X4), rhs_scale=v_s[h][:], start=True, stop=True)
+                nc.tensor.matmul_mx(
+                    out=h2[:], lhsT=w2_w[:, 2 * i * P : 2 * (i + 1) * P].bitcast(FP4X4),
+                    lhsT_scale=w2_s[:, i * P : (i + 1) * P], **moving,
+                )
+                for acc, which in ((h1, 0), (h3, 1)):
+                    codes, scales = wq[which, a]
+                    nc.tensor.matmul_mx(
+                        out=acc[:], lhsT=codes[:, cols].bitcast(FP8X4), lhsT_scale=scales[:, cols], **moving
+                    )
+                prod = keep.tile([P, BANK], F32, name="prod")
+                total = keep.tile([P, BANK], F32, name="total")
+                h2_sb = ring.tile([P, BANK], F32, name="h2_sb")
+                if (i, h) == (0, 0):
+                    nc.scalar.copy(out=h2_sb[:], in_=h2[:])
+                    nc.vector.scalar_tensor_tensor(prod[:], h3[:], gain_col, h2_sb[:], ALU.mult, ALU.mult)
+                    nc.vector.scalar_tensor_tensor(total[:], h1[:], gain_col, prod[:], ALU.mult, ALU.add)
+                    nc.vector.tensor_tensor(h_tile[:, half(h)], total[:], weights[:, half(h)], ALU.mult)
+                else:
+                    h1_sb = ring.tile([P, BANK], F32, name="h1_sb")
+                    h3_sb = ring.tile([P, BANK], F32, name="h3_sb")
+                    nc.scalar.activation(out=h2_sb[:], in_=h2[:], func=ACT.Copy, scale=gain_col)
+                    nc.scalar.copy(out=h3_sb[:], in_=h3[:])
+                    nc.scalar.activation(out=h1_sb[:], in_=h1[:], func=ACT.Copy, scale=gain_col)
+                    nc.gpsimd.tensor_tensor(prod[:], h2_sb[:], h3_sb[:], ALU.mult)
+                    nc.gpsimd.tensor_tensor(total[:], prod[:], h1_sb[:], ALU.add)
+                    nc.gpsimd.tensor_tensor(h_tile[:, half(h)], total[:], weights[:, half(h)], ALU.mult)
+            return h_tile
+
+        def put_into_page(i, h_tile):
+            if i < 2:
+                for h in range(2):
+                    nc.vector.tensor_copy(pages[i][:].indirect(list_half(idx2, h)), h_tile[:, half(h)])
+            else:
+                nc.vector.tensor_copy(pages[i][:].indirect(idx2[:]), h_tile[:])
+
+        def add_bias(dst, src, i):
+            a, t = divmod(i, PACK)
+            nc.scalar.activation(out=dst[:, :, t], in_=src, func=ACT.Identity, bias=b_t[:, a, t : t + 1])
+
+        def quantise_x(grouped, width, name):
+            codes = keep.tile([P, width], U32, name=name + "_w", align_bytes=64)
+            scales = keep.tile([P, width], U8, name=name + "_s", align_bytes=64)
+            nc.vector.quantize_mx(
+                out=codes[:].bitcast(FP8X4), scales=scales[:], in_=grouped[:].rearrange("p m t -> p (m t)")
+            )
+            return codes, scales
+
+        x_grouped0 = keep.tile([P, M, PACK], BF16, align_bytes=64)
+        x_grouped1 = [keep.tile([P, BANK, PACK], BF16, name="x_grouped1%d" % h, tag="x_grouped1%d" % h, align_bytes=64) for h in range(2)]
+
+        quantise_weight(0, 0, 0, 1, nc.scalar.copy)
+        quantise_weight(1, 0, 0, 1, nc.vector.tensor_copy)
+        for i in range(ROW_TILES):
+            if i == 1:
+                quantise_weight(0, 0, 1, PACK, nc.scalar.copy)
+                quantise_weight(1, 0, 1, PACK, nc.scalar.copy)
+            if i == 3:
+                deal_w2_scales(1)
+                quantise_weight(0, 1, 0, PACK, nc.scalar.copy)
+                quantise_weight(1, 1, 0, PACK, nc.scalar.copy)
+            if i >= 6:
+                pages.append(load_page(page0_rows[i // PACK, i % PACK], "page0_%d" % i, "page0"))
+            h_now = first_stage(i)
+            put_into_page(i, h_now)
+            picked = ring.tile([P, M], F32, name="picked")
+            if i < PACK:
+                nc.vector.tensor_copy(picked[:], pages[i][:].indirect(idx3[:]))
+                add_bias(x_grouped0, picked[:], i)
+            else:
+                nc.vector.tensor_copy(picked[:, half(0)], pages[i][:].indirect(list_half(idx3, 0)))
+                add_bias(x_grouped1[0], picked[:, half(0)], i)
+            if i == PACK - 1:
+                xq0 = quantise_x(x_grouped0, M, "xq0")
+
+        outs = [load_page(page1[n * P : (n + 1) * P, :], "page1_%d" % n, "big") for n in range(OUT_TILES)]
+
+        def second_stage(h, xq1):
+            for n in range(OUT_TILES):
+                cols = slice(n * P, (n + 1) * P)
+                e = psum.tile([P, BANK], F32, name="e")
+                nc.tensor.matmul_mx(
+                    out=e[:], lhsT=w4_w[:, 0, cols].bitcast(FP8X4), lhsT_scale=w4_s[:, 0, cols],
+                    rhs=xq0[0][:, half(h)].bitcast(FP8X4), rhs_scale=xq0[1][:, half(h)], start=True, stop=False,
+                )
+                nc.tensor.matmul_mx(
+                    out=e[:], lhsT=w4_w[:, 1, cols].bitcast(FP8X4), lhsT_scale=w4_s[:, 1, cols],
+                    rhs=xq1[0][:].bitcast(FP8X4), rhs_scale=xq1[1][:], start=False, stop=True,
+                )
+                mag = ring.tile([P, BANK], F32, name="mag", tag="h1_sb")
+                nc.scalar.activation(out=mag[:], in_=e[:], func=ACT.Abs)
+                y = ring.tile([P, BANK], F32, name="y", tag="h2_sb" if n % 2 == 0 else "h3_sb")
+                nc.scalar.activation(out=y[:], in_=mag[:], func=ACT.Ln, bias=1.0)
+                nc.vector.tensor_tensor(outs[n][:].indirect(list_half(idx4, h)), y[:], wgo_t[:, half(h)], ALU.mult)
+                if h == 1:
+                    nc.sync.dma_start(out=out[n * P : (n + 1) * P, :], in_=outs[n][:])
+
+        xq1_first = quantise_x(x_grouped1[0], BANK, "xq10")
+        late_pairs = [
+            keep.tile([P, 2, BANK], F32, name="late_a", tag="h_tile1"),
+            keep.tile([P, 2, BANK], F32, name="late_b", tag="x_grouped10", align_bytes=64),
+        ]
+        late = [late_pairs[t // 2][:, t % 2, :] for t in range(PACK)]
+        for t in range(PACK):
+            nc.vector.tensor_copy(late[t], pages[PACK + t][:].indirect(list_half(idx3, 1)))
+        second_stage(0, xq1_first)
+        for t in range(PACK):
+            add_bias(x_grouped1[1], late[t], PACK + t)
+        second_stage(1, quantise_x(x_grouped1[1], BANK, "xq11"))

@@ -31,7 +31,6 @@ def tile_list_cellar_transfer_page_kernel(
     nc = tc.nc
     with ExitStack() as ctx:
         keep = ctx.enter_context(tc.tile_pool(name="keep", bufs=1))
-        ring = ctx.enter_context(tc.tile_pool(name="ring", bufs=2))
         psum = ctx.enter_context(tc.psum_pool(name="psum", bufs=2))
 
         def half(h):
@@ -45,68 +44,76 @@ def tile_list_cellar_transfer_page_kernel(
             nc.sync.dma_start(tile[:], src)
             return tile
 
-        def load_scale_rows(queue, tile, src):
-            for q in range(4):
+        def load_scale_rows(queue, tile, src, quadrants=range(4)):
+            for q in quadrants:
                 queue.dma_start(
                     out=tile[32 * q : 32 * q + 4].bitcast(I32),
                     in_=src[:, 4 * q : 4 * q + 4, :].rearrange("a q c -> q a c").bitcast(I32),
                 )
 
-        def load_weight_half(src, a, name):
-            raw = ring.tile([P, PACK, BANK], F32, name=name, tag="big", bufs=6)
+        def load_weight_half(src, a, name, tag):
+            raw = keep.tile([P, PACK, BANK], F32, name=name, tag=tag)
             nc.sync.dma_start(out=raw[:], in_=src[:, half(a)].rearrange("(p i) c -> p i c", i=PACK))
             return raw
 
         def load_page(src, name, tag):
-            tile = ring.tile([P, T2], F32, name=name, tag=tag, bufs=6)
+            tile = keep.tile([P, T2], F32, name=name, tag=tag)
             nc.sync.dma_start(out=tile[:], in_=src)
             return tile
 
         page0_rows = page0.rearrange("(a p t) c -> a t p c", a=2, t=PACK)
         wgs_rows = wgs.rearrange("(p t) j -> p t j", t=PACK)
 
+        def load_wgs(t):
+            tile = keep.tile([P, S], F32, name="wgs%d" % t)
+            for q in range(4):
+                nc.sync.dma_start(out=tile[32 * q : 32 * q + 32, :], in_=wgs_rows[:, t, :])
+            return tile
+
         tab_s = keep.tile([P, 1, T], U8, align_bytes=64)
         nc.vector.memset(tab_s[:].bitcast(I32), 0)
         w2_s_raw = keep.tile([P, 1, H], U8, align_bytes=64)
         nc.gpsimd.memset(w2_s_raw[:].bitcast(I32), 0)
-        gain_t = keep.tile([P, 2, PACK], F32)
-        nc.gpsimd.dma_start(out=gain_t[:], in_=gain.rearrange("(a p t) -> p a t", a=2, t=PACK))
-        b_t = keep.tile([P, 2, PACK], F32)
-        nc.gpsimd.dma_start(out=b_t[:], in_=b.rearrange("(a p t) -> p a t", a=2, t=PACK))
+        load_scale_rows(nc.gpsimd, w2_s_raw, w2_scales, range(0, 2))
         w4_s = keep.tile([P, 2, N], U8, align_bytes=64)
         nc.gpsimd.memset(w4_s[:].bitcast(I32), 0)
 
         idx1 = load_list(offs, "idx1")
         w2_raw = keep.tile([P, 2 * H], U8, align_bytes=64)
         nc.sync.dma_start(out=w2_raw[:].bitcast(I32), in_=w2_words[0].bitcast(I32))
-        tab_w = keep.tile([P, T], U32, align_bytes=64)
-        nc.sync.dma_start(out=tab_w[:].bitcast(I32), in_=tab_words[0].rearrange("p t i -> p (t i)").bitcast(I32))
-        load_scale_rows(nc.sync, tab_s, tab_scales)
-        raw = {}
-        raw[0, 0] = load_weight_half(w1, 0, "w1_raw0")
-        load_scale_rows(nc.sync, w2_s_raw, w2_scales)
-        raw[1, 0] = load_weight_half(w3, 0, "w3_raw0")
-        wgs_first = keep.tile([P, S], F32)
-        for q in range(4):
-            nc.sync.dma_start(out=wgs_first[32 * q : 32 * q + 32, :], in_=wgs_rows[:, 0, :])
         idx2 = load_list(offs2, "idx2")
-        pages = [load_page(page0_rows[0, 0], "page0_0", "page0")]
-        wgs_rest = keep.tile([P, PACK - 1, S], F32, tag="wgs_rest")
-        for q in range(4):
-            nc.sync.dma_start(out=wgs_rest[32 * q : 32 * q + 32], in_=wgs_rows[:, 1:PACK, :])
-        pages.append(load_page(page0_rows[0, 1], "page0_1", "page0"))
         idx3 = load_list(offs3, "idx3")
-        pages.append(load_page(page0_rows[0, 2], "page0_2", "page0"))
-        raw[0, 1] = load_weight_half(w1, 1, "w1_raw1")
-        raw[1, 1] = load_weight_half(w3, 1, "w3_raw1")
-        for i in range(3, 6):
-            pages.append(load_page(page0_rows[i // PACK, i % PACK], "page0_%d" % i, "page0"))
+        idx4 = load_list(offs4, "idx4")
+        gain_t = keep.tile([P, 2, PACK], F32)
+        nc.sync.dma_start(out=gain_t[:], in_=gain.rearrange("(a p t) -> p a t", a=2, t=PACK))
+        b_t = keep.tile([P, 2, PACK], F32)
+        nc.sync.dma_start(out=b_t[:], in_=b.rearrange("(a p t) -> p a t", a=2, t=PACK))
+        raw = {}
+        raw[0, 0] = load_weight_half(w1, 0, "w1_raw0", "big2")
+        load_scale_rows(nc.sync, tab_s, tab_scales)
+        load_scale_rows(nc.sync, w2_s_raw, w2_scales, range(2, 4))
+        raw[1, 0] = load_weight_half(w3, 0, "w3_raw0", "big3")
+        tab_w = keep.tile([P, T], U32, tag="tab_w", align_bytes=64)
+        nc.sync.dma_start(out=tab_w[:].bitcast(I32), in_=tab_words[0].rearrange("p t i -> p (t i)").bitcast(I32))
+        wgs_t = []
+        pages = []
+        wgs_t.append(load_wgs(0))
+        wgs_t.append(load_wgs(1))
+        pages.append(load_page(page0_rows[0, 0], "page0_0", "page0"))
+        pages.append(load_page(page0_rows[0, 1], "page0_1", "page1"))
+        raw[0, 1] = load_weight_half(w1, 1, "w1_raw1", "big4")
+        wgs_t.append(load_wgs(2))
+        raw[1, 1] = load_weight_half(w3, 1, "w3_raw1", "big5")
+        wgs_t.append(load_wgs(3))
+        pages.append(load_page(page0_rows[0, 2], "page0_2", "page2"))
+        pages.append(load_page(page0_rows[0, 3], "page0_3", "page3"))
+        pages.append(load_page(page0_rows[1, 0], "page0_4", "page4"))
+        pages.append(load_page(page0_rows[1, 1], "page0_5", "page5"))
         w4_w = keep.tile([P, 2, N], U32, align_bytes=64)
         nc.sync.dma_start(out=w4_w[:].bitcast(I32), in_=w4_words.rearrange("a p c i -> p a (c i)").bitcast(I32))
-        load_scale_rows(nc.sync, w4_s, w4_scales)
         wgo_t = keep.tile([P, M], F32)
         nc.sync.dma_start(out=wgo_t[:], in_=wgo)
-        idx4 = load_list(offs4, "idx4")
+        load_scale_rows(nc.sync, w4_s, w4_scales)
 
         w2_w = keep.tile([P, 2 * H], U8, align_bytes=64)
         nc.vector.tensor_copy(
@@ -114,48 +121,58 @@ def tile_list_cellar_transfer_page_kernel(
             in_=w2_raw[:].rearrange("p (a m t e) -> p a t m e", a=2, t=PACK, e=2),
         )
         w2_s = keep.tile([P, H], U8, align_bytes=64)
-
-        def deal_w2_scales(a):
-            nc.vector.tensor_copy(
+        for a in range(2):
+            nc.gpsimd.tensor_copy(
                 out=w2_s[:, half(a)].rearrange("p (t m) -> p t m", t=PACK),
                 in_=w2_s_raw[:, 0, half(a)].rearrange("p (m t) -> p t m", t=PACK),
             )
 
+        def round_weights(a, tag):
+            rounded = keep.tile([P, 2, PACK, P, PACK], BF16, name="rounded%d" % a, tag=tag, align_bytes=64)
+            for which in range(2):
+                nc.scalar.copy(
+                    out=rounded[:, which].rearrange("p t m i -> p m t i"),
+                    in_=raw[which, a][:].rearrange("p i (m t) -> p m t i", t=PACK),
+                )
+            return rounded
+
+        def quantise_weights(a, rounded, tag):
+            codes = keep.tile([P, 2, BANK], U32, name="wq_w%d" % a, tag=tag, align_bytes=64)
+            scales = keep.tile([P, 2, BANK], U8, name="wq_s%d" % a, align_bytes=64)
+            for which in range(2):
+                nc.vector.quantize_mx(
+                    out=codes[:, which, :].bitcast(FP8X4),
+                    scales=scales[:, which, :],
+                    in_=rounded[:, which].rearrange("p t m i -> p (t m i)"),
+                )
+            return codes, scales
+
         v_w = [keep.tile([P, BANK], U32, name="v_w%d" % h, align_bytes=64) for h in range(2)]
         v_s = [keep.tile([P, BANK], U8, name="v_s%d" % h, align_bytes=64) for h in range(2)]
         for h in range(2):
-            nc.vector.tensor_copy(v_w[h][:], tab_w[:].indirect(list_half(idx1, h)))
             nc.vector.tensor_copy(v_s[h][:], tab_s[:, 0, :].indirect(list_half(idx1, h)))
-            if h == 0:
-                deal_w2_scales(0)
+        wq = [quantise_weights(0, round_weights(0, "x_rows0"), "wq_first")]
+        for h in range(2):
+            nc.vector.tensor_copy(v_w[h][:], tab_w[:].indirect(list_half(idx1, h)))
 
-        wq = {}
+        h_tags = ["h_even", "wq_second", "h_odd", "h_third", "h_even", "h_odd", "xq0_w", "h_third"]
 
-        for which in range(2):
-            for a in range(2):
-                wq[which, a] = (
-                    keep.tile([P, BANK], U32, name="wq_w%d%d" % (which, a), align_bytes=64),
-                    keep.tile([P, BANK], U8, name="wq_s%d%d" % (which, a), align_bytes=64),
-                )
+        work = keep.tile([P, S], F32)
 
-        def quantise_weight(which, a, t0, t1, copy):
-            grouped = ring.tile([P, t1 - t0, P, PACK], BF16, name="w_grouped%d" % min(t1 - t0, 2), align_bytes=64)
-            codes, scales = wq[which, a]
-            src = raw[which, a][:].rearrange("p i (m t) -> p t m i", t=PACK)
-            for t in range(t0, t1):
-                copy(out=grouped[:, t - t0], in_=src[:, t])
-            nc.vector.quantize_mx(
-                out=codes[:, t0 * P : t1 * P].bitcast(FP8X4),
-                scales=scales[:, t0 * P : t1 * P],
-                in_=grouped[:].rearrange("p t m i -> p (t m i)"),
-            )
+        def combine(dst, c1, c2, c3, weights, product, total):
+            nc.gpsimd.tensor_tensor(product, c2, c3, ALU.mult)
+            nc.gpsimd.tensor_tensor(total, c1, product, ALU.add)
+            nc.gpsimd.tensor_tensor(dst, total, weights, ALU.mult)
 
         def first_stage(i):
             a, t = divmod(i, PACK)
-            weights = wgs_first[:] if t == 0 else wgs_rest[:, t - 1, :]
-            h_tile = keep.tile([P, S], F32, name="h_tile", tag="h_tile%d" % (i % 2))
+            weights = wgs_t[t][:]
+            h_tile = keep.tile([P, S], F32, name="h_tile", tag=h_tags[i], align_bytes=64)
             cols = slice(t * P, (t + 1) * P)
             gain_col = gain_t[:, a, t : t + 1]
+            h1_sb = keep.tile([P, S], F32, name="h1_sb", tag="stage%d" % (i % 3))
+            h2_sb = keep.tile([P, S], F32, name="h2_sb", tag="h2_sb%d" % (i % 2), align_bytes=64)
+            h3_sb = keep.tile([P, S], F32, name="h3_sb", tag="h3_sb%d" % (i % 2), align_bytes=64)
             for h in range(2):
                 h1 = psum.tile([P, BANK], F32, name="h1")
                 h2 = psum.tile([P, BANK], F32, name="h2")
@@ -166,31 +183,30 @@ def tile_list_cellar_transfer_page_kernel(
                     lhsT_scale=w2_s[:, i * P : (i + 1) * P], **moving,
                 )
                 for acc, which in ((h1, 0), (h3, 1)):
-                    codes, scales = wq[which, a]
+                    codes, scales = wq[a]
                     nc.tensor.matmul_mx(
-                        out=acc[:], lhsT=codes[:, cols].bitcast(FP8X4), lhsT_scale=scales[:, cols], **moving
+                        out=acc[:], lhsT=codes[:, which, cols].bitcast(FP8X4), lhsT_scale=scales[:, which, cols],
+                        **moving,
                     )
-                prod = keep.tile([P, BANK], F32, name="prod")
-                total = keep.tile([P, BANK], F32, name="total")
-                h2_sb = ring.tile([P, BANK], F32, name="h2_sb")
-                if (i, h) == (0, 0):
-                    nc.scalar.copy(out=h2_sb[:], in_=h2[:])
-                    nc.vector.scalar_tensor_tensor(prod[:], h3[:], gain_col, h2_sb[:], ALU.mult, ALU.mult)
-                    nc.vector.scalar_tensor_tensor(total[:], h1[:], gain_col, prod[:], ALU.mult, ALU.add)
-                    nc.vector.tensor_tensor(h_tile[:, half(h)], total[:], weights[:, half(h)], ALU.mult)
+                c1, c2, c3 = h1_sb[:, half(h)], h2_sb[:, half(h)], h3_sb[:, half(h)]
+                if i == 0:
+                    nc.scalar.copy(out=c2, in_=h2[:])
+                    nc.vector.scalar_tensor_tensor(c3, h3[:], gain_col, c2, ALU.mult, ALU.mult)
+                    nc.vector.scalar_tensor_tensor(c1, h1[:], gain_col, c3, ALU.mult, ALU.add)
+                    nc.vector.tensor_tensor(h_tile[:, half(h)], c1, weights[:, half(h)], ALU.mult)
                 else:
-                    h1_sb = ring.tile([P, BANK], F32, name="h1_sb")
-                    h3_sb = ring.tile([P, BANK], F32, name="h3_sb")
-                    nc.scalar.activation(out=h2_sb[:], in_=h2[:], func=ACT.Copy, scale=gain_col)
-                    nc.scalar.copy(out=h3_sb[:], in_=h3[:])
-                    nc.scalar.activation(out=h1_sb[:], in_=h1[:], func=ACT.Copy, scale=gain_col)
-                    nc.gpsimd.tensor_tensor(prod[:], h2_sb[:], h3_sb[:], ALU.mult)
-                    nc.gpsimd.tensor_tensor(total[:], prod[:], h1_sb[:], ALU.add)
-                    nc.gpsimd.tensor_tensor(h_tile[:, half(h)], total[:], weights[:, half(h)], ALU.mult)
+                    nc.scalar.activation(out=c2, in_=h2[:], func=ACT.Copy, scale=gain_col)
+                    nc.scalar.copy(out=c3, in_=h3[:])
+                    nc.scalar.activation(out=c1, in_=h1[:], func=ACT.Copy, scale=gain_col)
+                    if i < 2:
+                        combine(h_tile[:, half(h)], c1, c2, c3, weights[:, half(h)], work[:, half(h)], work[:, half(h)])
+            if i >= 2:
+                product, total = (work, work) if i < PACK else (h2_sb, h1_sb)
+                combine(h_tile[:], h1_sb[:], h2_sb[:], h3_sb[:], weights, product[:], total[:])
             return h_tile
 
         def put_into_page(i, h_tile):
-            if i < 2:
+            if i == 1:
                 for h in range(2):
                     nc.vector.tensor_copy(pages[i][:].indirect(list_half(idx2, h)), h_tile[:, half(h)])
             else:
@@ -198,74 +214,101 @@ def tile_list_cellar_transfer_page_kernel(
 
         def add_bias(dst, src, i):
             a, t = divmod(i, PACK)
-            nc.scalar.activation(out=dst[:, :, t], in_=src, func=ACT.Identity, bias=b_t[:, a, t : t + 1])
+            nc.scalar.activation(out=dst, in_=src, func=ACT.Identity, bias=b_t[:, a, t : t + 1])
 
         def quantise_x(grouped, width, name):
-            codes = keep.tile([P, width], U32, name=name + "_w", align_bytes=64)
+            codes = keep.tile([P, width], U32, name=name + "_w", tag=name + "_w", align_bytes=64)
             scales = keep.tile([P, width], U8, name=name + "_s", align_bytes=64)
             nc.vector.quantize_mx(
                 out=codes[:].bitcast(FP8X4), scales=scales[:], in_=grouped[:].rearrange("p m t -> p (m t)")
             )
             return codes, scales
 
-        x_grouped0 = keep.tile([P, M, PACK], BF16, align_bytes=64)
-        x_grouped1 = [keep.tile([P, BANK, PACK], BF16, name="x_grouped1%d" % h, tag="x_grouped1%d" % h, align_bytes=64) for h in range(2)]
+        x_first = keep.tile([P, BANK, PACK], BF16, tag="x_first", align_bytes=64)
 
-        quantise_weight(0, 0, 0, 1, nc.scalar.copy)
-        quantise_weight(1, 0, 0, 1, nc.vector.tensor_copy)
-        for i in range(ROW_TILES):
-            if i == 1:
-                quantise_weight(0, 0, 1, PACK, nc.scalar.copy)
-                quantise_weight(1, 0, 1, PACK, nc.scalar.copy)
-            if i == 3:
-                deal_w2_scales(1)
-                quantise_weight(0, 1, 0, PACK, nc.scalar.copy)
-                quantise_weight(1, 1, 0, PACK, nc.scalar.copy)
-            if i >= 6:
-                pages.append(load_page(page0_rows[i // PACK, i % PACK], "page0_%d" % i, "page0"))
-            h_now = first_stage(i)
-            put_into_page(i, h_now)
-            picked = ring.tile([P, M], F32, name="picked")
+        def fetch_from_page(i):
+            picked = keep.tile([P, M], F32, name="picked", tag="stage%d" % ((i + 1) % 3))
             if i < PACK:
                 nc.vector.tensor_copy(picked[:], pages[i][:].indirect(idx3[:]))
-                add_bias(x_grouped0, picked[:], i)
+                add_bias(x_rows0[:, i, :], picked[:], i)
             else:
                 nc.vector.tensor_copy(picked[:, half(0)], pages[i][:].indirect(list_half(idx3, 0)))
-                add_bias(x_grouped1[0], picked[:, half(0)], i)
-            if i == PACK - 1:
-                xq0 = quantise_x(x_grouped0, M, "xq0")
+                add_bias(x_first[:, :, i - PACK], picked[:, half(0)], i)
 
-        outs = [load_page(page1[n * P : (n + 1) * P, :], "page1_%d" % n, "big") for n in range(OUT_TILES)]
+        h_tiles = [first_stage(0)]
+        for i in range(ROW_TILES):
+            if i == ROW_TILES - 1:
+                fetch_from_page(i - 1)
+            put_into_page(i, h_tiles[i])
+            if i == 0:
+                h_tiles.append(first_stage(1))
+            if i == 1:
+                wq.append(quantise_weights(1, round_weights(1, "x_rows0"), "wq_second"))
+                x_rows0 = keep.tile([P, PACK, M], BF16, tag="x_rows0", align_bytes=64)
+            if i + 2 < ROW_TILES:
+                h_tiles.append(first_stage(i + 2))
+            if 0 < i < ROW_TILES - 1:
+                fetch_from_page(i - 1)
+            if i in (1, 2):
+                pages.append(load_page(page0_rows[1, i + 1], "page0_%d" % (i + 5), "page%d" % (i - 1)))
+            if i == ROW_TILES - 2:
+                xq0_w = keep.tile([P, M], U32, tag="xq0_w", align_bytes=64)
+                xq0_s = keep.tile([P, M], U8, align_bytes=64)
+                for h, tag in enumerate(("h2_sb0", "h3_sb0")):
+                    x_grouped = keep.tile([P, BANK, PACK], BF16, name="x_grouped", tag=tag, align_bytes=64)
+                    nc.scalar.copy(
+                        out=x_grouped[:].rearrange("p (c i) t -> p c t i", i=4),
+                        in_=x_rows0[:, :, half(h)].rearrange("p t (c i) -> p c t i", i=4),
+                    )
+                    nc.vector.quantize_mx(
+                        out=xq0_w[:, half(h)].bitcast(FP8X4), scales=xq0_s[:, half(h)],
+                        in_=x_grouped[:].rearrange("p m t -> p (m t)"),
+                    )
+                xq0 = (xq0_w, xq0_s)
+        fetch_from_page(ROW_TILES - 1)
 
-        def second_stage(h, xq1):
-            for n in range(OUT_TILES):
-                cols = slice(n * P, (n + 1) * P)
-                e = psum.tile([P, BANK], F32, name="e")
-                nc.tensor.matmul_mx(
-                    out=e[:], lhsT=w4_w[:, 0, cols].bitcast(FP8X4), lhsT_scale=w4_s[:, 0, cols],
-                    rhs=xq0[0][:, half(h)].bitcast(FP8X4), rhs_scale=xq0[1][:, half(h)], start=True, stop=False,
-                )
-                nc.tensor.matmul_mx(
-                    out=e[:], lhsT=w4_w[:, 1, cols].bitcast(FP8X4), lhsT_scale=w4_s[:, 1, cols],
-                    rhs=xq1[0][:].bitcast(FP8X4), rhs_scale=xq1[1][:], start=False, stop=True,
-                )
-                mag = ring.tile([P, BANK], F32, name="mag", tag="h1_sb")
-                nc.scalar.activation(out=mag[:], in_=e[:], func=ACT.Abs)
-                y = ring.tile([P, BANK], F32, name="y", tag="h2_sb" if n % 2 == 0 else "h3_sb")
-                nc.scalar.activation(out=y[:], in_=mag[:], func=ACT.Ln, bias=1.0)
-                nc.vector.tensor_tensor(outs[n][:].indirect(list_half(idx4, h)), y[:], wgo_t[:, half(h)], ALU.mult)
-                if h == 1:
-                    nc.sync.dma_start(out=out[n * P : (n + 1) * P, :], in_=outs[n][:])
+        outs = [load_page(page1[n * P : (n + 1) * P, :], "page1_%d" % n, "big%d" % n) for n in range(OUT_TILES)]
 
-        xq1_first = quantise_x(x_grouped1[0], BANK, "xq10")
+        y_tags = ["stage0", "stage1", "stage2"]
+
+        def second_stage(h, xq1, n):
+            cols = slice(n * P, (n + 1) * P)
+            e = psum.tile([P, BANK], F32, name="e")
+            nc.tensor.matmul_mx(
+                out=e[:], lhsT=w4_w[:, 0, cols].bitcast(FP8X4), lhsT_scale=w4_s[:, 0, cols],
+                rhs=xq0[0][:, half(h)].bitcast(FP8X4), rhs_scale=xq0[1][:, half(h)], start=True, stop=False,
+            )
+            nc.tensor.matmul_mx(
+                out=e[:], lhsT=w4_w[:, 1, cols].bitcast(FP8X4), lhsT_scale=w4_s[:, 1, cols],
+                rhs=xq1[0][:].bitcast(FP8X4), rhs_scale=xq1[1][:], start=False, stop=True,
+            )
+            mag_tag = "h3_sb1" if (h, n) == (0, 0) else "h2_sb%d" % (n % 2)
+            mag = keep.tile([P, BANK], F32, name="mag", tag=mag_tag, align_bytes=64)
+            nc.scalar.activation(out=mag[:], in_=e[:], func=ACT.Abs)
+            if (h, n) == (0, 3):
+                y = keep.tile([P, BANK], F32, name="y", tag="xq11_w", align_bytes=64)
+            else:
+                y = keep.tile([P, BANK], F32, name="y", tag=y_tags[n % 3])
+            nc.scalar.activation(out=y[:], in_=mag[:], func=ACT.Ln, bias=1.0)
+            nc.vector.tensor_tensor(outs[n][:].indirect(list_half(idx4, h)), y[:], wgo_t[:, half(h)], ALU.mult)
+            if h == 1:
+                nc.sync.dma_start(out=out[n * P : (n + 1) * P, :], in_=outs[n][:])
+
+        xq1_first = quantise_x(x_first, BANK, "xq10")
         late_pairs = [
-            keep.tile([P, 2, BANK], F32, name="late_a", tag="h_tile1"),
-            keep.tile([P, 2, BANK], F32, name="late_b", tag="x_grouped10", align_bytes=64),
+            keep.tile([P, 2, BANK], F32, name="late_a", tag="h_third", align_bytes=64),
+            keep.tile([P, 2, BANK], F32, name="late_b", tag="x_first", align_bytes=64),
         ]
         late = [late_pairs[t // 2][:, t % 2, :] for t in range(PACK)]
         for t in range(PACK):
             nc.vector.tensor_copy(late[t], pages[PACK + t][:].indirect(list_half(idx3, 1)))
-        second_stage(0, xq1_first)
+        for n in range(4):
+            second_stage(0, xq1_first, n)
+        x_second = keep.tile([P, BANK, PACK], BF16, tag="h3_sb1", align_bytes=64)
         for t in range(PACK):
-            add_bias(x_grouped1[1], late[t], PACK + t)
-        second_stage(1, quantise_x(x_grouped1[1], BANK, "xq11"))
+            add_bias(x_second[:, :, t], late[t], PACK + t)
+        xq1_second = quantise_x(x_second, BANK, "xq11")
+        for n in range(4, OUT_TILES):
+            second_stage(0, xq1_first, n)
+        for n in range(OUT_TILES):
+            second_stage(1, xq1_second, n)

@@ -81,34 +81,34 @@ def tile_list_cellar_transfer_page_kernel(
         idx1 = load_list(offs, "idx1")
         w2_raw = keep.tile([P, 2 * H], U8, align_bytes=64)
         nc.sync.dma_start(out=w2_raw[:].bitcast(I32), in_=w2_words[0].bitcast(I32))
-        idx2 = load_list(offs2, "idx2")
-        idx3 = load_list(offs3, "idx3")
-        idx4 = load_list(offs4, "idx4")
-        gain_t = keep.tile([P, 2, PACK], F32)
-        nc.sync.dma_start(out=gain_t[:], in_=gain.rearrange("(a p t) -> p a t", a=2, t=PACK))
-        b_t = keep.tile([P, 2, PACK], F32)
-        nc.sync.dma_start(out=b_t[:], in_=b.rearrange("(a p t) -> p a t", a=2, t=PACK))
         raw = {}
         raw[0, 0] = load_weight_half(w1, 0, "w1_raw0", "big2")
         load_scale_rows(nc.sync, tab_s, tab_scales)
-        load_scale_rows(nc.sync, w2_s_raw, w2_scales, range(2, 4))
         raw[1, 0] = load_weight_half(w3, 0, "w3_raw0", "big3")
+        load_scale_rows(nc.sync, w2_s_raw, w2_scales, range(2, 4))
         tab_w = keep.tile([P, T], U32, tag="tab_w", align_bytes=64)
         nc.sync.dma_start(out=tab_w[:].bitcast(I32), in_=tab_words[0].rearrange("p t i -> p (t i)").bitcast(I32))
+        gain_t = keep.tile([P, 2, PACK], F32)
+        nc.sync.dma_start(out=gain_t[:], in_=gain.rearrange("(a p t) -> p a t", a=2, t=PACK))
+        idx2 = load_list(offs2, "idx2")
         wgs_t = []
         pages = []
         wgs_t.append(load_wgs(0))
-        wgs_t.append(load_wgs(1))
         pages.append(load_page(page0_rows[0, 0], "page0_0", "page0"))
+        wgs_t.append(load_wgs(1))
         pages.append(load_page(page0_rows[0, 1], "page0_1", "page1"))
+        idx3 = load_list(offs3, "idx3")
         raw[0, 1] = load_weight_half(w1, 1, "w1_raw1", "big4")
         wgs_t.append(load_wgs(2))
         raw[1, 1] = load_weight_half(w3, 1, "w3_raw1", "big5")
         wgs_t.append(load_wgs(3))
+        b_t = keep.tile([P, 2, PACK], F32)
+        nc.sync.dma_start(out=b_t[:], in_=b.rearrange("(a p t) -> p a t", a=2, t=PACK))
         pages.append(load_page(page0_rows[0, 2], "page0_2", "page2"))
         pages.append(load_page(page0_rows[0, 3], "page0_3", "page3"))
         pages.append(load_page(page0_rows[1, 0], "page0_4", "page4"))
         pages.append(load_page(page0_rows[1, 1], "page0_5", "page5"))
+        idx4 = load_list(offs4, "idx4")
         w4_w = keep.tile([P, 2, N], U32, align_bytes=64)
         nc.sync.dma_start(out=w4_w[:].bitcast(I32), in_=w4_words.rearrange("a p c i -> p a (c i)").bitcast(I32))
         wgo_t = keep.tile([P, M], F32)
@@ -136,14 +136,14 @@ def tile_list_cellar_transfer_page_kernel(
                 )
             return rounded
 
-        def quantise_weights(a, rounded, tag):
+        def quantise_weights(a, rounded, tag, calls):
             codes = keep.tile([P, 2, BANK], U32, name="wq_w%d" % a, tag=tag, align_bytes=64)
             scales = keep.tile([P, 2, BANK], U8, name="wq_s%d" % a, align_bytes=64)
-            for which in range(2):
+            for w0, w1_ in calls:
                 nc.vector.quantize_mx(
-                    out=codes[:, which, :].bitcast(FP8X4),
-                    scales=scales[:, which, :],
-                    in_=rounded[:, which].rearrange("p t m i -> p (t m i)"),
+                    out=codes[:, w0:w1_, :].rearrange("p w c -> p (w c)").bitcast(FP8X4),
+                    scales=scales[:, w0:w1_, :].rearrange("p w c -> p (w c)"),
+                    in_=rounded[:, w0:w1_].rearrange("p w t m i -> p (w t m i)"),
                 )
             return codes, scales
 
@@ -151,7 +151,7 @@ def tile_list_cellar_transfer_page_kernel(
         v_s = [keep.tile([P, BANK], U8, name="v_s%d" % h, align_bytes=64) for h in range(2)]
         for h in range(2):
             nc.vector.tensor_copy(v_s[h][:], tab_s[:, 0, :].indirect(list_half(idx1, h)))
-        wq = [quantise_weights(0, round_weights(0, "x_rows0"), "wq_first")]
+        wq = [quantise_weights(0, round_weights(0, "x_rows0"), "wq_first", [(0, 1), (1, 2)])]
         for h in range(2):
             nc.vector.tensor_copy(v_w[h][:], tab_w[:].indirect(list_half(idx1, h)))
 
@@ -170,7 +170,8 @@ def tile_list_cellar_transfer_page_kernel(
             h_tile = keep.tile([P, S], F32, name="h_tile", tag=h_tags[i], align_bytes=64)
             cols = slice(t * P, (t + 1) * P)
             gain_col = gain_t[:, a, t : t + 1]
-            h1_sb = keep.tile([P, S], F32, name="h1_sb", tag="stage%d" % (i % 3))
+            if i > 0:
+                h1_sb = keep.tile([P, S], F32, name="h1_sb", tag="stage%d" % (i % 3))
             h2_sb = keep.tile([P, S], F32, name="h2_sb", tag="h2_sb%d" % (i % 2), align_bytes=64)
             h3_sb = keep.tile([P, S], F32, name="h3_sb", tag="h3_sb%d" % (i % 2), align_bytes=64)
             for h in range(2):
@@ -188,13 +189,14 @@ def tile_list_cellar_transfer_page_kernel(
                         out=acc[:], lhsT=codes[:, which, cols].bitcast(FP8X4), lhsT_scale=scales[:, which, cols],
                         **moving,
                     )
-                c1, c2, c3 = h1_sb[:, half(h)], h2_sb[:, half(h)], h3_sb[:, half(h)]
+                c2, c3 = h2_sb[:, half(h)], h3_sb[:, half(h)]
                 if i == 0:
                     nc.scalar.copy(out=c2, in_=h2[:])
                     nc.vector.scalar_tensor_tensor(c3, h3[:], gain_col, c2, ALU.mult, ALU.mult)
-                    nc.vector.scalar_tensor_tensor(c1, h1[:], gain_col, c3, ALU.mult, ALU.add)
-                    nc.vector.tensor_tensor(h_tile[:, half(h)], c1, weights[:, half(h)], ALU.mult)
+                    nc.vector.scalar_tensor_tensor(work[:, half(h)], h1[:], gain_col, c3, ALU.mult, ALU.add)
+                    nc.vector.tensor_tensor(h_tile[:, half(h)], work[:, half(h)], weights[:, half(h)], ALU.mult)
                 else:
+                    c1 = h1_sb[:, half(h)]
                     nc.scalar.activation(out=c2, in_=h2[:], func=ACT.Copy, scale=gain_col)
                     nc.scalar.copy(out=c3, in_=h3[:])
                     nc.scalar.activation(out=c1, in_=h1[:], func=ACT.Copy, scale=gain_col)
@@ -243,7 +245,7 @@ def tile_list_cellar_transfer_page_kernel(
             if i == 0:
                 h_tiles.append(first_stage(1))
             if i == 1:
-                wq.append(quantise_weights(1, round_weights(1, "x_rows0"), "wq_second"))
+                wq.append(quantise_weights(1, round_weights(1, "x_rows0"), "wq_second", [(0, 2)]))
                 x_rows0 = keep.tile([P, PACK, M], BF16, tag="x_rows0", align_bytes=64)
             if i + 2 < ROW_TILES:
                 h_tiles.append(first_stage(i + 2))
@@ -282,7 +284,7 @@ def tile_list_cellar_transfer_page_kernel(
                 out=e[:], lhsT=w4_w[:, 1, cols].bitcast(FP8X4), lhsT_scale=w4_s[:, 1, cols],
                 rhs=xq1[0][:].bitcast(FP8X4), rhs_scale=xq1[1][:], start=False, stop=True,
             )
-            mag_tag = "h3_sb1" if (h, n) == (0, 0) else "h2_sb%d" % (n % 2)
+            mag_tag = "h3_sb1" if h == 0 and n < 2 else "h2_sb%d" % (n % 2)
             mag = keep.tile([P, BANK], F32, name="mag", tag=mag_tag, align_bytes=64)
             nc.scalar.activation(out=mag[:], in_=e[:], func=ACT.Abs)
             if (h, n) == (0, 3):
@@ -292,14 +294,13 @@ def tile_list_cellar_transfer_page_kernel(
             nc.scalar.activation(out=y[:], in_=mag[:], func=ACT.Ln, bias=1.0)
             nc.vector.tensor_tensor(outs[n][:].indirect(list_half(idx4, h)), y[:], wgo_t[:, half(h)], ALU.mult)
             if h == 1:
-                nc.sync.dma_start(out=out[n * P : (n + 1) * P, :], in_=outs[n][:])
+                queue = nc.scalar if n == OUT_TILES - 1 else nc.sync
+                queue.dma_start(out=out[n * P : (n + 1) * P, :], in_=outs[n][:])
 
         xq1_first = quantise_x(x_first, BANK, "xq10")
-        late_pairs = [
-            keep.tile([P, 2, BANK], F32, name="late_a", tag="h_third", align_bytes=64),
-            keep.tile([P, 2, BANK], F32, name="late_b", tag="x_first", align_bytes=64),
-        ]
-        late = [late_pairs[t // 2][:, t % 2, :] for t in range(PACK)]
+        late_one = keep.tile([P, BANK], F32, tag="h_third", align_bytes=64)
+        late_rest = keep.tile([P, PACK - 1, BANK], F32, tag="x_first", align_bytes=64)
+        late = [late_one[:]] + [late_rest[:, t, :] for t in range(PACK - 1)]
         for t in range(PACK):
             nc.vector.tensor_copy(late[t], pages[PACK + t][:].indirect(list_half(idx3, 1)))
         for n in range(4):

@@ -98,8 +98,8 @@ def tile_list_cellar_transfer_page_kernel(
         wgs_t.append(load_wgs(1))
         pages.append(load_page(page0_rows[0, 1], "page0_1", "page1"))
         idx3 = load_list(offs3, "idx3")
-        raw[0, 1] = load_weight_half(w1, 1, "w1_raw1", "big4")
         wgs_t.append(load_wgs(2))
+        raw[0, 1] = load_weight_half(w1, 1, "w1_raw1", "big4")
         raw[1, 1] = load_weight_half(w3, 1, "w3_raw1", "big5")
         wgs_t.append(load_wgs(3))
         b_t = keep.tile([P, 2, PACK], F32)
@@ -175,9 +175,10 @@ def tile_list_cellar_transfer_page_kernel(
             h2_sb = keep.tile([P, S], F32, name="h2_sb", tag="h2_sb%d" % (i % 2), align_bytes=64)
             h3_sb = keep.tile([P, S], F32, name="h3_sb", tag="h3_sb%d" % (i % 2), align_bytes=64)
             for h in range(2):
-                h1 = psum.tile([P, BANK], F32, name="h1")
-                h2 = psum.tile([P, BANK], F32, name="h2")
-                h3 = psum.tile([P, BANK], F32, name="h3")
+                h2, h3, h1 = [
+                    psum.tile([P, BANK], F32, name="h_sum", tag="bank%d%d" % (h, (role + i) % 3), bufs=1)
+                    for role in range(3)
+                ]
                 moving = dict(rhs=v_w[h][:].bitcast(FP8X4), rhs_scale=v_s[h][:], start=True, stop=True)
                 nc.tensor.matmul_mx(
                     out=h2[:], lhsT=w2_w[:, 2 * i * P : 2 * (i + 1) * P].bitcast(FP4X4),

from contextlib import ExitStack

import concourse.mybir as mybir

K, T, S, H, T2, M, N = 512, 4096, 1024, 1024, 2048, 1024, 768
FLOPS = 2 * 3 * K * H * S + 2 * H * N * M

F32 = mybir.dt.float32
BF16 = mybir.dt.bfloat16
I32 = mybir.dt.int32
U32 = mybir.dt.uint32
U16 = mybir.dt.uint16
U8 = mybir.dt.uint8
FP8X4 = mybir.dt.float8_e4m3fn_x4
FP4X4 = mybir.dt.float4_e2m1fn_x4
ALU = mybir.AluOpType
ACT = mybir.ActivationFunctionType

P = 128
PACK = 4
BANK = 512
LIST_COLS = BANK // 16
ROW_TILES = H // P
OUT_TILES = N // P


def tile_list_cellar_transfer_page_kernel(
    tc, tab_words, tab_scales, offs, offs2, offs3, offs4, w1, w2_words, w2_scales, w3, gain, wgs, page0, b,
    w4_words, w4_scales, wgo, page1, out,
):
    nc = tc.nc
    with ExitStack() as ctx:
        keep = ctx.enter_context(tc.tile_pool(name="keep", bufs=1))
        psum = ctx.enter_context(tc.psum_pool(name="psum", bufs=2))

        def half(h):
            return slice(h * BANK, (h + 1) * BANK)

        def list_half(tile, h):
            return tile[:, h * LIST_COLS : (h + 1) * LIST_COLS]

        def load_list(src, name):
            tile = keep.tile([P, S // 16], U16, name=name)
            nc.sync.dma_start(tile[:], src)
            return tile

        def load_scale_rows(queue, tile, src, quadrants=range(4)):
            for q in quadrants:
                queue.dma_start(
                    out=tile[32 * q : 32 * q + 4].bitcast(I32),
                    in_=src[:, 4 * q : 4 * q + 4, :].rearrange("a q c -> q a c").bitcast(I32),
                )

        def load_weight_half(src, a, name, tag):
            raw = keep.tile([P, PACK, BANK], F32, name=name, tag=tag)
            nc.sync.dma_start(out=raw[:], in_=src[:, half(a)].rearrange("(p i) c -> p i c", i=PACK))
            return raw

        def load_page(src, name, tag):
            tile = keep.tile([P, T2], F32, name=name, tag=tag)
            nc.sync.dma_start(out=tile[:], in_=src)
            return tile

        page0_rows = page0.rearrange("(a p t) c -> a t p c", a=2, t=PACK)
        wgs_rows = wgs.rearrange("(p t) j -> p t j", t=PACK)

        def load_wgs(t):
            tile = keep.tile([P, S], F32, name="wgs%d" % t)
            for q in range(4):
                nc.sync.dma_start(out=tile[32 * q : 32 * q + 32, :], in_=wgs_rows[:, t, :])
            return tile

        tab_s = keep.tile([P, 1, T], U8, align_bytes=64)
        nc.vector.memset(tab_s[:].bitcast(I32), 0)
        w2_s_raw = keep.tile([P, 1, H], U8, align_bytes=64)
        nc.gpsimd.memset(w2_s_raw[:].bitcast(I32), 0)
        load_scale_rows(nc.gpsimd, w2_s_raw, w2_scales, range(0, 2))
        w4_s = keep.tile([P, 2, N], U8, align_bytes=64)
        nc.gpsimd.memset(w4_s[:].bitcast(I32), 0)

        idx1 = load_list(offs, "idx1")
        w2_raw = keep.tile([P, 2 * H], U8, align_bytes=64)
        nc.sync.dma_start(out=w2_raw[:].bitcast(I32), in_=w2_words[0].bitcast(I32))
        raw = {}
        raw[0, 0] = load_weight_half(w1, 0, "w1_raw0", "big2")
        load_scale_rows(nc.sync, tab_s, tab_scales)
        raw[1, 0] = load_weight_half(w3, 0, "w3_raw0", "big3")
        load_scale_rows(nc.sync, w2_s_raw, w2_scales, range(2, 4))
        tab_w = keep.tile([P, T], U32, tag="tab_w", align_bytes=64)
        nc.sync.dma_start(out=tab_w[:].bitcast(I32), in_=tab_words[0].rearrange("p t i -> p (t i)").bitcast(I32))
        gain_t = keep.tile([P, 2, PACK], F32)
        nc.sync.dma_start(out=gain_t[:], in_=gain.rearrange("(a p t) -> p a t", a=2, t=PACK))
        idx2 = load_list(offs2, "idx2")
        wgs_t = []
        pages = []
        wgs_t.append(load_wgs(0))
        pages.append(load_page(page0_rows[0, 0], "page0_0", "page0"))
        wgs_t.append(load_wgs(1))
        pages.append(load_page(page0_rows[0, 1], "page0_1", "page1"))
        idx3 = load_list(offs3, "idx3")
        wgs_t.append(load_wgs(2))
        raw[0, 1] = load_weight_half(w1, 1, "w1_raw1", "big4")
        raw[1, 1] = load_weight_half(w3, 1, "w3_raw1", "big5")
        wgs_t.append(load_wgs(3))
        b_t = keep.tile([P, 2, PACK], F32)
        nc.sync.dma_start(out=b_t[:], in_=b.rearrange("(a p t) -> p a t", a=2, t=PACK))
        pages.append(load_page(page0_rows[0, 2], "page0_2", "page2"))
        pages.append(load_page(page0_rows[0, 3], "page0_3", "page3"))
        pages.append(load_page(page0_rows[1, 0], "page0_4", "page4"))
        pages.append(load_page(page0_rows[1, 1], "page0_5", "page5"))
        idx4 = load_list(offs4, "idx4")
        w4_w = keep.tile([P, 2, N], U32, align_bytes=64)
        nc.sync.dma_start(out=w4_w[:].bitcast(I32), in_=w4_words.rearrange("a p c i -> p a (c i)").bitcast(I32))
        wgo_t = keep.tile([P, M], F32)
        nc.sync.dma_start(out=wgo_t[:], in_=wgo)
        load_scale_rows(nc.sync, w4_s, w4_scales)

        w2_w = keep.tile([P, 2 * H], U8, align_bytes=64)
        nc.vector.tensor_copy(
            out=w2_w[:].rearrange("p (a t m e) -> p a t m e", a=2, t=PACK, e=2),
            in_=w2_raw[:].rearrange("p (a m t e) -> p a t m e", a=2, t=PACK, e=2),
        )
        w2_s = keep.tile([P, H], U8, align_bytes=64)
        for a in range(2):
            nc.gpsimd.tensor_copy(
                out=w2_s[:, half(a)].rearrange("p (t m) -> p t m", t=PACK),
                in_=w2_s_raw[:, 0, half(a)].rearrange("p (m t) -> p t m", t=PACK),
            )

        def round_weights(a, tag):
            rounded = keep.tile([P, 2, PACK, P, PACK], BF16, name="rounded%d" % a, tag=tag, align_bytes=64)
            for which in range(2):
                nc.scalar.copy(
                    out=rounded[:, which].rearrange("p t m i -> p m t i"),
                    in_=raw[which, a][:].rearrange("p i (m t) -> p m t i", t=PACK),
                )
            return rounded

        def quantise_weights(a, rounded, tag, calls):
            codes = keep.tile([P, 2, BANK], U32, name="wq_w%d" % a, tag=tag, align_bytes=64)
            scales = keep.tile([P, 2, BANK], U8, name="wq_s%d" % a, align_bytes=64)
            for w0, w1_ in calls:
                nc.vector.quantize_mx(
                    out=codes[:, w0:w1_, :].rearrange("p w c -> p (w c)").bitcast(FP8X4),
                    scales=scales[:, w0:w1_, :].rearrange("p w c -> p (w c)"),
                    in_=rounded[:, w0:w1_].rearrange("p w t m i -> p (w t m i)"),
                )
            return codes, scales

        v_w = [keep.tile([P, BANK], U32, name="v_w%d" % h, align_bytes=64) for h in range(2)]
        v_s = [keep.tile([P, BANK], U8, name="v_s%d" % h, align_bytes=64) for h in range(2)]
        for h in range(2):
            nc.vector.tensor_copy(v_s[h][:], tab_s[:, 0, :].indirect(list_half(idx1, h)))
        wq = [quantise_weights(0, round_weights(0, "x_rows0"), "wq_first", [(0, 1), (1, 2)])]
        for h in range(2):
            nc.vector.tensor_copy(v_w[h][:], tab_w[:].indirect(list_half(idx1, h)))

        h_tags = ["h_even", "wq_second", "h_odd", "h_third", "h_even", "h_odd", "xq0_w", "h_third"]

        work = keep.tile([P, S], F32)

        def combine(dst, c1, c2, c3, weights, product, total):
            nc.gpsimd.tensor_tensor(product, c2, c3, ALU.mult)
            nc.gpsimd.tensor_tensor(total, c1, product, ALU.add)
            nc.gpsimd.tensor_tensor(dst, total, weights, ALU.mult)

        def first_stage(i):
            a, t = divmod(i, PACK)
            weights = wgs_t[t][:]
            h_tile = keep.tile([P, S], F32, name="h_tile", tag=h_tags[i], align_bytes=64)
            cols = slice(t * P, (t + 1) * P)
            gain_col = gain_t[:, a, t : t + 1]
            if i > 0:
                h1_sb = keep.tile([P, S], F32, name="h1_sb", tag="stage%d" % (i % 3))
            h2_sb = keep.tile([P, S], F32, name="h2_sb", tag="h2_sb%d" % (i % 2), align_bytes=64)
            h3_sb = keep.tile([P, S], F32, name="h3_sb", tag="h3_sb%d" % (i % 2), align_bytes=64)
            for h in range(2):
                h2, h3, h1 = [
                    psum.tile([P, BANK], F32, name="h_sum", tag="bank%d%d" % (h, (role + i) % 3), bufs=1)
                    for role in range(3)
                ]
                moving = dict(rhs=v_w[h][:].bitcast(FP8X4), rhs_scale=v_s[h][:], start=True, stop=True)
                nc.tensor.matmul_mx(
                    out=h2[:], lhsT=w2_w[:, 2 * i * P : 2 * (i + 1) * P].bitcast(FP4X4),
                    lhsT_scale=w2_s[:, i * P : (i + 1) * P], **moving,
                )
                for acc, which in ((h1, 0), (h3, 1)):
                    codes, scales = wq[a]
                    nc.tensor.matmul_mx(
                        out=acc[:], lhsT=codes[:, which, cols].bitcast(FP8X4), lhsT_scale=scales[:, which, cols],
                        **moving,
                    )
                c2, c3 = h2_sb[:, half(h)], h3_sb[:, half(h)]
                if i == 0:
                    nc.scalar.copy(out=c2, in_=h2[:])
                    nc.vector.scalar_tensor_tensor(c3, h3[:], gain_col, c2, ALU.mult, ALU.mult)
                    nc.vector.scalar_tensor_tensor(work[:, half(h)], h1[:], gain_col, c3, ALU.mult, ALU.add)
                    nc.vector.tensor_tensor(h_tile[:, half(h)], work[:, half(h)], weights[:, half(h)], ALU.mult)
                else:
                    c1 = h1_sb[:, half(h)]
                    nc.scalar.activation(out=c2, in_=h2[:], func=ACT.Copy, scale=gain_col)
                    nc.scalar.copy(out=c3, in_=h3[:])
                    nc.scalar.activation(out=c1, in_=h1[:], func=ACT.Copy, scale=gain_col)
                    if i < 2:
                        combine(h_tile[:, half(h)], c1, c2, c3, weights[:, half(h)], work[:, half(h)], work[:, half(h)])
            if i >= 2:
                product, total = (work, work) if i < PACK else (h2_sb, h1_sb)
                combine(h_tile[:], h1_sb[:], h2_sb[:], h3_sb[:], weights, product[:], total[:])
            return h_tile

        def put_into_page(i, h_tile):
            if i == 1:
                for h in range(2):
                    nc.vector.tensor_copy(pages[i][:].indirect(list_half(idx2, h)), h_tile[:, half(h)])
            else:
                nc.vector.tensor_copy(pages[i][:].indirect(idx2[:]), h_tile[:])

        def add_bias(dst, src, i):
            a, t = divmod(i, PACK)
            nc.scalar.activation(out=dst, in_=src, func=ACT.Identity, bias=b_t[:, a, t : t + 1])

        def quantise_x(grouped, width, name):
            codes = keep.tile([P, width], U32, name=name + "_w", tag=name + "_w", align_bytes=64)
            scales = keep.tile([P, width], U8, name=name + "_s", align_bytes=64)
            nc.vector.quantize_mx(
                out=codes[:].bitcast(FP8X4), scales=scales[:], in_=grouped[:].rearrange("p m t -> p (m t)")
            )
            return codes, scales

        x_first = keep.tile([P, BANK, PACK], BF16, tag="x_first", align_bytes=64)

        def fetch_from_page(i):
            picked = keep.tile([P, M], F32, name="picked", tag="stage%d" % ((i + 1) % 3))
            if i < PACK:
                nc.vector.tensor_copy(picked[:], pages[i][:].indirect(idx3[:]))
                add_bias(x_rows0[:, i, :], picked[:], i)
            else:
                nc.vector.tensor_copy(picked[:, half(0)], pages[i][:].indirect(list_half(idx3, 0)))
                add_bias(x_first[:, :, i - PACK], picked[:, half(0)], i)

        h_tiles = [first_stage(0)]
        for i in range(ROW_TILES):
            if i == ROW_TILES - 1:
                fetch_from_page(i - 1)
            put_into_page(i, h_tiles[i])
            if i == 0:
                h_tiles.append(first_stage(1))
            if i == 1:
                wq.append(quantise_weights(1, round_weights(1, "x_rows0"), "wq_second", [(0, 2)]))
                x_rows0 = keep.tile([P, PACK, M], BF16, tag="x_rows0", align_bytes=64)
            if i + 2 < ROW_TILES:
                h_tiles.append(first_stage(i + 2))
            if 0 < i < ROW_TILES - 1:
                fetch_from_page(i - 1)
            if i in (1, 2):
                pages.append(load_page(page0_rows[1, i + 1], "page0_%d" % (i + 5), "page%d" % (i - 1)))
            if i == ROW_TILES - 2:
                xq0_w = keep.tile([P, M], U32, tag="xq0_w", align_bytes=64)
                xq0_s = keep.tile([P, M], U8, align_bytes=64)
                for h, tag in enumerate(("h2_sb0", "h3_sb0")):
                    x_grouped = keep.tile([P, BANK, PACK], BF16, name="x_grouped", tag=tag, align_bytes=64)
                    nc.scalar.copy(
                        out=x_grouped[:].rearrange("p (c i) t -> p c t i", i=4),
                        in_=x_rows0[:, :, half(h)].rearrange("p t (c i) -> p c t i", i=4),
                    )
                    nc.vector.quantize_mx(
                        out=xq0_w[:, half(h)].bitcast(FP8X4), scales=xq0_s[:, half(h)],
                        in_=x_grouped[:].rearrange("p m t -> p (m t)"),
                    )
                xq0 = (xq0_w, xq0_s)
        fetch_from_page(ROW_TILES - 1)

        outs = [load_page(page1[n * P : (n + 1) * P, :], "page1_%d" % n, "big%d" % n) for n in range(OUT_TILES)]

        y_tags = ["stage0", "stage1", "stage2"]

        def second_stage(h, xq1, n):
            cols = slice(n * P, (n + 1) * P)
            e = psum.tile([P, BANK], F32, name="e")
            nc.tensor.matmul_mx(
                out=e[:], lhsT=w4_w[:, 0, cols].bitcast(FP8X4), lhsT_scale=w4_s[:, 0, cols],
                rhs=xq0[0][:, half(h)].bitcast(FP8X4), rhs_scale=xq0[1][:, half(h)], start=True, stop=False,
            )
            nc.tensor.matmul_mx(
                out=e[:], lhsT=w4_w[:, 1, cols].bitcast(FP8X4), lhsT_scale=w4_s[:, 1, cols],
                rhs=xq1[0][:].bitcast(FP8X4), rhs_scale=xq1[1][:], start=False, stop=True,
            )
            mag_tag = "h3_sb1" if h == 0 and n < 2 else "h2_sb%d" % (n % 2)
            mag = keep.tile([P, BANK], F32, name="mag", tag=mag_tag, align_bytes=64)
            nc.scalar.activation(out=mag[:], in_=e[:], func=ACT.Abs)
            if (h, n) == (0, 3):
                y = keep.tile([P, BANK], F32, name="y", tag="xq11_w", align_bytes=64)
            else:
                y = keep.tile([P, BANK], F32, name="y", tag=y_tags[n % 3])
            nc.scalar.activation(out=y[:], in_=mag[:], func=ACT.Ln, bias=1.0)
            nc.vector.tensor_tensor(outs[n][:].indirect(list_half(idx4, h)), y[:], wgo_t[:, half(h)], ALU.mult)
            if h == 1:
                queue = nc.scalar if n == OUT_TILES - 1 else nc.sync
                queue.dma_start(out=out[n * P : (n + 1) * P, :], in_=outs[n][:])

        xq1_first = quantise_x(x_first, BANK, "xq10")
        late_one = keep.tile([P, BANK], F32, tag="h_third", align_bytes=64)
        late_rest = keep.tile([P, PACK - 1, BANK], F32, tag="x_first", align_bytes=64)
        late = [late_one[:]] + [late_rest[:, t, :] for t in range(PACK - 1)]
        for t in range(PACK):
            nc.vector.tensor_copy(late[t], pages[PACK + t][:].indirect(list_half(idx3, 1)))
        for n in range(4):
            second_stage(0, xq1_first, n)
        x_second = keep.tile([P, BANK, PACK], BF16, tag="h3_sb1", align_bytes=64)
        for t in range(PACK):
            add_bias(x_second[:, :, t], late[t], PACK + t)
        xq1_second = quantise_x(x_second, BANK, "xq11")
        for n in range(4, OUT_TILES):
            second_stage(0, xq1_first, n)
        for n in range(OUT_TILES):
            second_stage(1, xq1_second, n)
